import numpy as np
import ml_dtypes


def mxq(x, axis, fmt="e4m3"):
    dtype, down = {"e4m3": (ml_dtypes.float8_e4m3fn, 7), "e5m2": (ml_dtypes.float8_e5m2, 14)}[fmt]
    v = np.moveaxis(np.asarray(x, np.float32).astype(ml_dtypes.bfloat16).astype(np.float64), axis, -1)
    blocks = v.reshape(v.shape[:-1] + (-1, 32))
    amax = np.abs(blocks).max(-1, keepdims=True)
    byte = np.maximum(np.where(amax > 0, np.frexp(amax)[1] - 1 + 127, 0) - down, 1)
    scale = np.exp2(byte - 127.0)
    codes = (blocks / scale).astype(np.float32).astype(dtype).astype(np.float64)
    return np.moveaxis((codes * scale).reshape(v.shape), -1, axis)


WIDE = False


def mx_kscale(k):
    if not WIDE:
        return np.ones(k)
    levels = np.array([10, -10, 5, -5, 0])
    if k % 512:
        return np.exp2(np.random.permutation(np.resize(levels, k // 32))).repeat(32)
    a = np.empty((k // 512, 16))
    for p in range(k // 512):
        a[p, :8] = np.random.permutation(np.resize(levels, 8))
        for g in range(8):
            far = levels[np.abs(levels - a[p, g]) >= 10]
            a[p, g + 8] = far[np.random.randint(len(far))]
    return np.exp2(a.ravel()).repeat(32)


def f64(x):
    return np.asarray(x).astype(np.float64)


def striped(idx):
    return np.tile(idx.reshape(-1, 16).T, (8, 1)).astype(np.uint16)


def unstriped(offs):
    return offs[:16].T.reshape(-1).astype(np.int64)


def pack_weight(w):
    k, n = w.shape
    w = f64(np.asarray(w, np.float32).astype(ml_dtypes.bfloat16)).reshape(k // 32, 32, n)
    amax = np.abs(w).max(1)
    byte = np.clip(np.where(amax > 0, np.frexp(amax)[1] - 1 + 127 - 7, 1), 1, 254)
    scaled = (w * np.exp2(127.0 - byte)[:, None, :]).reshape(k, n).astype(np.float32)
    words = np.ascontiguousarray(scaled.reshape(k // 512, 128, 4, n).transpose(0, 1, 3, 2)).astype(ml_dtypes.float8_e4m3fn).view(np.uint8)
    return words, np.ascontiguousarray(byte.astype(np.uint8).reshape(k // 512, 16, n))


def unpack_weight(words, scales):
    g, p, n, _ = words.shape
    vals = np.ascontiguousarray(words).view(ml_dtypes.float8_e4m3fn).astype(np.float64) * np.repeat(np.exp2(scales.astype(np.float64) - 127.0), 8, axis=1)[..., None]
    return vals.transpose(0, 1, 3, 2).reshape(g * 512, n)


K, T, S, V, D = 512, 2048, 512, 512, 8


def setup_inputs():
    n = np.random.standard_normal
    s = mx_kscale(K)[:, None]
    packed_xT = pack_weight(n((K, T)) * s)
    return {
        "x_words": packed_xT[0],
        "x_scales": packed_xT[1],
        "hT": (n((K, V)) / np.sqrt(K) / s).astype(np.float32),
        "jump": (np.random.uniform(0.2, 1.0, (V, S))).astype(np.float32),
        "offs": striped(np.random.permutation(T)[:S]),
    }


def reference(x_words, x_scales, hT, jump, offs):
    hTq = mxq(f64(hT), 0, "e4m3")
    xq = unpack_weight(x_words, x_scales)[:, unstriped(offs)]
    tp = np.exp(0.8 * (hTq.T @ xq))
    wt = tp * f64(jump)
    tot = wt.reshape(len(wt), -1, D).sum(axis=2) + 0.3
    post = wt / np.repeat(tot, D, axis=1)
    return post * np.log(20.0 * post + 1.0)

@@ -1,0 +1,176 @@
+from contextlib import ExitStack
+
+import concourse.mybir as mybir
+
+K, T, S, V, D = 512, 2048, 512, 512, 8
+FLOPS = 2 * K * V * S
+
+F32 = mybir.dt.float32
+BF16 = mybir.dt.bfloat16
+I32 = mybir.dt.int32
+U32 = mybir.dt.uint32
+U16 = mybir.dt.uint16
+U8 = mybir.dt.uint8
+FP8X4 = mybir.dt.float8_e4m3fn_x4
+ACT = mybir.ActivationFunctionType
+MULT = mybir.AluOpType.mult
+ADD = mybir.AluOpType.add
+
+P = 128
+PACK = 4
+TILES = V // P
+GROUPS = S // D
+PITCH = 16
+HALF = S // 2
+HG = GROUPS // 2
+
+
+def tile_picked_yibm1_post_p_kernel(tc, x_words, x_scales, hT, jump, offs, out):
+    nc = tc.nc
+    with ExitStack() as ctx:
+        keep = ctx.enter_context(tc.tile_pool(name="keep", bufs=1))
+        psum = ctx.enter_context(tc.psum_pool(name="psum", bufs=1))
+
+        offsets = keep.tile([P, S // 16], U16, name="offsets")
+        nc.sync.dma_start(offsets[:], offs)
+
+        scale_table = keep.tile([P, T], U8, name="scale_table", align_bytes=64)
+        nc.vector.memset(scale_table[:].bitcast(I32), 0)
+        for q in range(4):
+            nc.scalar.dma_start(
+                out=scale_table[32 * q : 32 * q + 4, :].bitcast(I32),
+                in_=x_scales[0, 4 * q : 4 * q + 4, :].bitcast(I32),
+            )
+
+        wts = [keep.tile([P, GROUPS, PITCH], F32, name=f"wt{b}", align_bytes=64) for b in range(2)]
+        zeros_a = keep.tile([P, GROUPS], F32, name="zeros_a", tag="words", align_bytes=64)
+        nc.vector.memset(zeros_a[:], 0.0)
+        zeros_b = keep.tile([P, GROUPS], F32, name="zeros_b", tag="jump")
+        nc.vector.memset(zeros_b[:], 0.0)
+        nc.vector.tensor_scalar(out=wts[0][:, :, D], in0=zeros_a[:], scalar1=0.3, scalar2=None, op0=ADD)
+        nc.scalar.activation(out=wts[1][:, :, D], in_=zeros_b[:], func=ACT.Copy, bias=0.3)
+
+        h_raw = keep.tile([P, PACK, V], F32, name="h_raw")
+        nc.sync.dma_start(out=h_raw[:], in_=hT.rearrange("(p j) t -> p j t", j=PACK))
+
+        word_table = keep.tile([P, T], U32, name="word_table", tag="words", align_bytes=64)
+        nc.sync.dma_start(
+            out=word_table[:].bitcast(I32),
+            in_=x_words[0].rearrange("p n r -> p (n r)").bitcast(I32),
+        )
+
+        jump_all = keep.tile([P, TILES, S], F32, name="jump_all", tag="jump")
+        nc.sync.dma_start(out=jump_all[:, 0, :], in_=jump[0:P, :])
+        nc.sync.dma_start(out=jump_all[:, 1:, :], in_=jump[P:, :].rearrange("(i p) s -> p i s", p=P))
+        jumps = [jump_all[:, i, :] for i in range(TILES)]
+
+        x_bytes = keep.tile([P, S], U8, name="x_bytes", align_bytes=64)
+        nc.vector.tensor_copy(out=x_bytes[:], in_=scale_table[:].indirect(offsets[:]))
+
+        h_codes, h_bytes = [], []
+        grouped = []
+        for i in range(TILES):
+            g = keep.tile([P, P, PACK], BF16, name=f"h_grouped{i}", align_bytes=64)
+            dst = g[:].rearrange("p (c e) j -> p c j e", e=4)
+            src = h_raw[:, :, i * P : (i + 1) * P].rearrange("p j (c e) -> p c j e", e=4)
+            if i % 2 == 0:
+                nc.vector.tensor_copy(out=dst, in_=src)
+            else:
+                nc.scalar.copy(out=dst, in_=src)
+            grouped.append(g)
+        for i in (0, 2, 1, 3):
+            codes = keep.tile([P, P], U32, name=f"h_codes{i}", align_bytes=64)
+            scales = keep.tile([P, P], U8, name=f"h_bytes{i}", align_bytes=64)
+            nc.vector.quantize_mx(
+                out=codes[:].bitcast(FP8X4), scales=scales[:], in_=grouped[i][:].rearrange("p c j -> p (c j)")
+            )
+            h_codes.append((i, codes))
+            h_bytes.append((i, scales))
+        h_codes = dict(h_codes)
+        h_bytes = dict(h_bytes)
+
+        x_codes = [keep.tile([P, HALF], U32, name=f"x_codes{u}", align_bytes=64) for u in range(2)]
+        for u in range(2):
+            nc.vector.tensor_copy(out=x_codes[u][:], in_=word_table[:].indirect(offsets[:, 16 * u : 16 * (u + 1)]))
+
+        tps = [None] + [keep.tile([P, GROUPS, D], F32, name=f"tp{i}") for i in range(1, TILES)]
+
+        def tp_view(i, u):
+            gs = slice(u * HG, (u + 1) * HG)
+            return wts[1][:, gs, 0:D] if i == 0 else tps[i][:, gs, :]
+
+        for i, u in ((0, 0), (1, 0), (0, 1), (1, 1), (2, 0), (2, 1), (3, 0), (3, 1)):
+            bank = psum.tile([P, HALF], F32, name=f"bank{i}{u}")
+            nc.tensor.matmul_mx(
+                out=bank[:],
+                lhsT=h_codes[i][:].bitcast(FP8X4),
+                lhsT_scale=h_bytes[i][:],
+                rhs=x_codes[u][:].bitcast(FP8X4),
+                rhs_scale=x_bytes[:, u * HALF : (u + 1) * HALF],
+                start=True,
+                stop=True,
+            )
+            nc.scalar.activation(
+                out=tp_view(i, u), in_=bank[:].rearrange("p (g d) -> p g d", d=D), func=ACT.Exp, scale=0.8
+            )
+
+        posts = [keep.tile([P, S], F32, name=f"post{i}") for i in range(TILES)]
+        logs = [keep.tile([P, S], F32, name=f"log{i}") for i in range(TILES)]
+        results = [wts[0][:, HG:, :].rearrange("p g e -> p (g e)")] + [
+            keep.tile([P, S], F32, name=f"result{i}")[:] for i in range(1, TILES)
+        ]
+
+        def weigh(i):
+            wt = wts[i % 2]
+            jv = jumps[i].rearrange("p (g d) -> p g d", d=D)
+            if i == 0:
+                for u in range(2):
+                    gs = slice(u * HG, (u + 1) * HG)
+                    nc.vector.tensor_tensor(out=wt[:, gs, 0:D], in0=tp_view(0, u), in1=jv[:, gs, :], op=MULT)
+            else:
+                nc.gpsimd.tensor_tensor(out=wt[:, :, 0:D], in0=tps[i][:], in1=jv, op=MULT)
+
+        def share(i):
+            wt = wts[i % 2]
+            tot = keep.tile([P, GROUPS], F32, name=f"tot{i}")
+            inv = keep.tile([P, GROUPS], F32, name=f"inv{i}")
+            halves = [slice(u * HG, (u + 1) * HG) for u in range(2)]
+            for gs in halves:
+                nc.vector.tensor_reduce(out=tot[:, gs], in_=wt[:, gs, 0 : D + 1], axis=mybir.AxisListType.X, op=ADD)
+            for gs in halves:
+                nc.vector.reciprocal(out=inv[:, gs], in_=tot[:, gs])
+            pv = posts[i][:].rearrange("p (g d) -> p g d", d=D)
+            for gs in halves:
+                nc.vector.tensor_tensor(
+                    out=pv[:, gs, :],
+                    in0=wt[:, gs, 0:D],
+                    in1=inv[:, gs].unsqueeze(2).to_broadcast([P, HG, D]),
+                    op=MULT,
+                )
+
+        def logarithm(i, cols):
+            nc.scalar.activation(out=logs[i][:, cols], in_=posts[i][:, cols], func=ACT.Ln, scale=20.0, bias=1.0)
+
+        def finish(i, cols, engine):
+            engine.tensor_tensor(out=results[i][:, cols], in0=posts[i][:, cols], in1=logs[i][:, cols], op=MULT)
+            nc.sync.dma_start(out=out[i * P : (i + 1) * P, cols], in_=results[i][:, cols])
+
+        whole = slice(0, S)
+        weigh(0)
+        weigh(1)
+        share(0)
+        logarithm(0, whole)
+        weigh(2)
+        share(1)
+        logarithm(1, whole)
+        weigh(3)
+        share(2)
+        logarithm(2, whole)
+        finish(0, whole, nc.gpsimd)
+        share(3)
+        for u in range(2):
+            logarithm(3, slice(u * HALF, (u + 1) * HALF))
+        finish(1, whole, nc.vector)
+        finish(2, whole, nc.vector)
+        for u in range(2):
+            finish(3, slice(u * HALF, (u + 1) * HALF), nc.vector)

@@ -42,13 +42,15 @@ def tile_picked_yibm1_post_p_kernel(tc, x_words, x_scales, hT, jump, offs, out):
                 in_=x_scales[0, 4 * q : 4 * q + 4, :].bitcast(I32),
             )
 
-        wts = [keep.tile([P, GROUPS, PITCH], F32, name=f"wt{b}", align_bytes=64) for b in range(2)]
+        wts = [keep.tile([P, GROUPS, PITCH], F32, name=f"wt{b}", align_bytes=64) for b in range(TILES)]
         zeros_a = keep.tile([P, GROUPS], F32, name="zeros_a", tag="words", align_bytes=64)
         nc.vector.memset(zeros_a[:], 0.0)
         zeros_b = keep.tile([P, GROUPS], F32, name="zeros_b", tag="jump")
         nc.vector.memset(zeros_b[:], 0.0)
         nc.vector.tensor_scalar(out=wts[0][:, :, D], in0=zeros_a[:], scalar1=0.3, scalar2=None, op0=ADD)
         nc.scalar.activation(out=wts[1][:, :, D], in_=zeros_b[:], func=ACT.Copy, bias=0.3)
+        for i in (2, 3):
+            nc.vector.tensor_scalar(out=wts[i][:, :, D], in0=zeros_b[:], scalar1=0.3, scalar2=None, op0=ADD)
 
         h_raw = keep.tile([P, PACK, V], F32, name="h_raw")
         nc.sync.dma_start(out=h_raw[:], in_=hT.rearrange("(p j) t -> p j t", j=PACK))
@@ -93,11 +95,8 @@ def tile_picked_yibm1_post_p_kernel(tc, x_words, x_scales, hT, jump, offs, out):
         for u in range(2):
             nc.vector.tensor_copy(out=x_codes[u][:], in_=word_table[:].indirect(offsets[:, 16 * u : 16 * (u + 1)]))
 
-        tps = [None] + [keep.tile([P, GROUPS, D], F32, name=f"tp{i}") for i in range(1, TILES)]
-
         def tp_view(i, u):
-            gs = slice(u * HG, (u + 1) * HG)
-            return wts[1][:, gs, 0:D] if i == 0 else tps[i][:, gs, :]
+            return wts[i][:, u * HG : (u + 1) * HG, 0:D]
 
         for i, u in ((0, 0), (1, 0), (0, 1), (1, 1), (2, 0), (2, 1), (3, 0), (3, 1)):
             bank = psum.tile([P, HALF], F32, name=f"bank{i}{u}")
@@ -116,37 +115,28 @@ def tile_picked_yibm1_post_p_kernel(tc, x_words, x_scales, hT, jump, offs, out):
 
         posts = [keep.tile([P, S], F32, name=f"post{i}") for i in range(TILES)]
         logs = [keep.tile([P, S], F32, name=f"log{i}") for i in range(TILES)]
-        results = [wts[0][:, HG:, :].rearrange("p g e -> p (g e)")] + [
-            keep.tile([P, S], F32, name=f"result{i}")[:] for i in range(1, TILES)
-        ]
+        results = [keep.tile([P, S], F32, name=f"result{i}")[:] for i in range(TILES)]
+        tots = [keep.tile([P, GROUPS], F32, name=f"tot{i}") for i in range(TILES)]
+        invs = [keep.tile([P, GROUPS], F32, name=f"inv{i}") for i in range(TILES)]
 
-        def weigh(i):
-            wt = wts[i % 2]
+        def weigh(i, gs):
             jv = jumps[i].rearrange("p (g d) -> p g d", d=D)
-            if i == 0:
-                for u in range(2):
-                    gs = slice(u * HG, (u + 1) * HG)
-                    nc.vector.tensor_tensor(out=wt[:, gs, 0:D], in0=tp_view(0, u), in1=jv[:, gs, :], op=MULT)
-            else:
-                nc.gpsimd.tensor_tensor(out=wt[:, :, 0:D], in0=tps[i][:], in1=jv, op=MULT)
+            nc.vector.tensor_tensor(out=wts[i][:, gs, 0:D], in0=wts[i][:, gs, 0:D], in1=jv[:, gs, :], op=MULT)
 
-        def share(i):
-            wt = wts[i % 2]
-            tot = keep.tile([P, GROUPS], F32, name=f"tot{i}")
-            inv = keep.tile([P, GROUPS], F32, name=f"inv{i}")
-            halves = [slice(u * HG, (u + 1) * HG) for u in range(2)]
-            for gs in halves:
-                nc.vector.tensor_reduce(out=tot[:, gs], in_=wt[:, gs, 0 : D + 1], axis=mybir.AxisListType.X, op=ADD)
-            for gs in halves:
-                nc.vector.reciprocal(out=inv[:, gs], in_=tot[:, gs])
+        def total(i, gs):
+            nc.vector.tensor_reduce(out=tots[i][:, gs], in_=wts[i][:, gs, 0 : D + 1], axis=mybir.AxisListType.X, op=ADD)
+
+        def invert(i, gs):
+            nc.vector.reciprocal(out=invs[i][:, gs], in_=tots[i][:, gs])
+
+        def share(i, gs):
             pv = posts[i][:].rearrange("p (g d) -> p g d", d=D)
-            for gs in halves:
-                nc.vector.tensor_tensor(
-                    out=pv[:, gs, :],
-                    in0=wt[:, gs, 0:D],
-                    in1=inv[:, gs].unsqueeze(2).to_broadcast([P, HG, D]),
-                    op=MULT,
-                )
+            nc.vector.tensor_tensor(
+                out=pv[:, gs, :],
+                in0=wts[i][:, gs, 0:D],
+                in1=invs[i][:, gs].unsqueeze(2).to_broadcast([P, gs.stop - gs.start, D]),
+                op=MULT,
+            )
 
         def logarithm(i, cols):
             nc.scalar.activation(out=logs[i][:, cols], in_=posts[i][:, cols], func=ACT.Ln, scale=20.0, bias=1.0)
@@ -156,20 +146,30 @@ def tile_picked_yibm1_post_p_kernel(tc, x_words, x_scales, hT, jump, offs, out):
             nc.sync.dma_start(out=out[i * P : (i + 1) * P, cols], in_=results[i][:, cols])
 
         whole = slice(0, S)
-        weigh(0)
-        weigh(1)
-        share(0)
+        every = slice(0, GROUPS)
+        halves = [slice(0, HG), slice(HG, GROUPS)]
+        weigh(0, halves[0])
+        weigh(0, halves[1])
+        weigh(1, every)
+        total(0, every)
+        total(1, every)
+        invert(0, every)
+        invert(1, every)
+        share(0, every)
         logarithm(0, whole)
-        weigh(2)
-        share(1)
+        weigh(2, every)
+        share(1, every)
         logarithm(1, whole)
-        weigh(3)
-        share(2)
+        weigh(3, every)
+        total(2, every)
+        total(3, every)
+        invert(2, every)
+        invert(3, every)
+        share(2, every)
         logarithm(2, whole)
-        finish(0, whole, nc.gpsimd)
-        share(3)
-        for u in range(2):
-            logarithm(3, slice(u * HALF, (u + 1) * HALF))
+        share(3, every)
+        logarithm(3, whole)
+        finish(0, whole, nc.vector)
         finish(1, whole, nc.vector)
         finish(2, whole, nc.vector)
         for u in range(2):

@@ -23,6 +23,7 @@ GROUPS = S // D
 PITCH = 16
 HALF = S // 2
 HG = GROUPS // 2
+EARLY = 4
 
 
 def tile_picked_yibm1_post_p_kernel(tc, x_words, x_scales, hT, jump, offs, out):
@@ -42,80 +43,73 @@ def tile_picked_yibm1_post_p_kernel(tc, x_words, x_scales, hT, jump, offs, out):
                 in_=x_scales[0, 4 * q : 4 * q + 4, :].bitcast(I32),
             )
 
-        wts = [keep.tile([P, GROUPS, PITCH], F32, name=f"wt{b}", align_bytes=64) for b in range(TILES)]
-        zeros_a = keep.tile([P, GROUPS], F32, name="zeros_a", tag="words", align_bytes=64)
-        nc.vector.memset(zeros_a[:], 0.0)
-        zeros_b = keep.tile([P, GROUPS], F32, name="zeros_b", tag="jump")
-        nc.vector.memset(zeros_b[:], 0.0)
-        nc.vector.tensor_scalar(out=wts[0][:, :, D], in0=zeros_a[:], scalar1=0.3, scalar2=None, op0=ADD)
-        nc.scalar.activation(out=wts[1][:, :, D], in_=zeros_b[:], func=ACT.Copy, bias=0.3)
-        for i in (2, 3):
-            nc.vector.tensor_scalar(out=wts[i][:, :, D], in0=zeros_b[:], scalar1=0.3, scalar2=None, op0=ADD)
+        wts = [keep.tile([P, GROUPS, PITCH], F32, name=f"wt{i}", align_bytes=64) for i in range(TILES)]
+        for i in range(TILES):
+            zeros = keep.tile([P, GROUPS], F32, name=f"zeros{i}", tag=f"late{i}", align_bytes=64)
+            nc.vector.memset(zeros[:], 0.0)
+            if i < TILES - 1:
+                nc.vector.tensor_scalar(out=wts[i][:, :, D], in0=zeros[:], scalar1=0.3, scalar2=None, op0=ADD)
+            else:
+                nc.scalar.activation(out=wts[i][:, :, D], in_=zeros[:], func=ACT.Copy, bias=0.3)
 
-        h_raw = keep.tile([P, PACK, V], F32, name="h_raw")
-        nc.sync.dma_start(out=h_raw[:], in_=hT.rearrange("(p j) t -> p j t", j=PACK))
-
-        word_table = keep.tile([P, T], U32, name="word_table", tag="words", align_bytes=64)
+        h_rows = hT.rearrange("(p j) t -> p j t", j=PACK)
+        jump_rows = jump.rearrange("(i p) s -> p i s", p=P)
+        h_early = keep.tile([P, PACK, EARLY * P], F32, name="h_early")
+        nc.sync.dma_start(out=h_early[:], in_=h_rows[:, :, 0 : EARLY * P])
+        word_table = keep.tile([P, T], U32, name="word_table", tag="late0", align_bytes=64)
         nc.sync.dma_start(
             out=word_table[:].bitcast(I32),
             in_=x_words[0].rearrange("p n r -> p (n r)").bitcast(I32),
         )
-
-        jump_all = keep.tile([P, TILES, S], F32, name="jump_all", tag="jump")
-        nc.sync.dma_start(out=jump_all[:, 0, :], in_=jump[0:P, :])
-        nc.sync.dma_start(out=jump_all[:, 1:, :], in_=jump[P:, :].rearrange("(i p) s -> p i s", p=P))
-        jumps = [jump_all[:, i, :] for i in range(TILES)]
+        jump_early = keep.tile([P, 2, S], F32, name="jump_early", tag="late1", align_bytes=64)
+        nc.sync.dma_start(out=jump_early[:], in_=jump_rows[:, 0:2, :])
+        jump_late = keep.tile([P, 2, S], F32, name="jump_late", tag="late3", align_bytes=64)
+        nc.sync.dma_start(out=jump_late[:], in_=jump_rows[:, 2:4, :])
+        h_raw = [h_early[:, :, i * P : (i + 1) * P] for i in range(EARLY)]
+        jumps = [jump_early[:, 0, :], jump_early[:, 1, :], jump_late[:, 0, :], jump_late[:, 1, :]]
 
         x_bytes = keep.tile([P, S], U8, name="x_bytes", align_bytes=64)
         nc.vector.tensor_copy(out=x_bytes[:], in_=scale_table[:].indirect(offsets[:]))
 
-        h_codes, h_bytes = [], []
-        grouped = []
-        for i in range(TILES):
-            g = keep.tile([P, P, PACK], BF16, name=f"h_grouped{i}", align_bytes=64)
-            dst = g[:].rearrange("p (c e) j -> p c j e", e=4)
-            src = h_raw[:, :, i * P : (i + 1) * P].rearrange("p j (c e) -> p c j e", e=4)
+        grouped = [keep.tile([P, P, PACK], BF16, name=f"h_grouped{i}", align_bytes=64) for i in range(TILES)]
+        h_codes = [keep.tile([P, P], U32, name=f"h_codes{i}", align_bytes=64) for i in range(TILES)]
+        h_bytes = [keep.tile([P, P], U8, name=f"h_bytes{i}", align_bytes=64) for i in range(TILES)]
+        x_codes = keep.tile([P, S], U32, name="x_codes", align_bytes=64)
+
+        def interleave(i):
+            dst = grouped[i][:].rearrange("p (c e) j -> p c j e", e=4)
+            src = h_raw[i].rearrange("p j (c e) -> p c j e", e=4)
             if i % 2 == 0:
                 nc.vector.tensor_copy(out=dst, in_=src)
             else:
                 nc.scalar.copy(out=dst, in_=src)
-            grouped.append(g)
-        for i in (0, 2, 1, 3):
-            codes = keep.tile([P, P], U32, name=f"h_codes{i}", align_bytes=64)
-            scales = keep.tile([P, P], U8, name=f"h_bytes{i}", align_bytes=64)
+
+        def quantize(i):
             nc.vector.quantize_mx(
-                out=codes[:].bitcast(FP8X4), scales=scales[:], in_=grouped[i][:].rearrange("p c j -> p (c j)")
+                out=h_codes[i][:].bitcast(FP8X4),
+                scales=h_bytes[i][:],
+                in_=grouped[i][:].rearrange("p c j -> p (c j)"),
             )
-            h_codes.append((i, codes))
-            h_bytes.append((i, scales))
-        h_codes = dict(h_codes)
-        h_bytes = dict(h_bytes)
 
-        x_codes = [keep.tile([P, HALF], U32, name=f"x_codes{u}", align_bytes=64) for u in range(2)]
-        for u in range(2):
-            nc.vector.tensor_copy(out=x_codes[u][:], in_=word_table[:].indirect(offsets[:, 16 * u : 16 * (u + 1)]))
-
-        def tp_view(i, u):
-            return wts[i][:, u * HG : (u + 1) * HG, 0:D]
-
-        for i, u in ((0, 0), (1, 0), (0, 1), (1, 1), (2, 0), (2, 1), (3, 0), (3, 1)):
-            bank = psum.tile([P, HALF], F32, name=f"bank{i}{u}")
+        def score(i, gs):
+            cols = slice(gs.start * D, gs.stop * D)
+            bank = psum.tile([P, cols.stop - cols.start], F32, name=f"bank{i}_{gs.start}")
             nc.tensor.matmul_mx(
                 out=bank[:],
                 lhsT=h_codes[i][:].bitcast(FP8X4),
                 lhsT_scale=h_bytes[i][:],
-                rhs=x_codes[u][:].bitcast(FP8X4),
-                rhs_scale=x_bytes[:, u * HALF : (u + 1) * HALF],
+                rhs=x_codes[:, cols].bitcast(FP8X4),
+                rhs_scale=x_bytes[:, cols],
                 start=True,
                 stop=True,
             )
             nc.scalar.activation(
-                out=tp_view(i, u), in_=bank[:].rearrange("p (g d) -> p g d", d=D), func=ACT.Exp, scale=0.8
+                out=wts[i][:, gs, 0:D], in_=bank[:].rearrange("p (g d) -> p g d", d=D), func=ACT.Exp, scale=0.8
             )
 
         posts = [keep.tile([P, S], F32, name=f"post{i}") for i in range(TILES)]
         logs = [keep.tile([P, S], F32, name=f"log{i}") for i in range(TILES)]
-        results = [keep.tile([P, S], F32, name=f"result{i}")[:] for i in range(TILES)]
+        results = [jumps[3], jumps[2]] + [keep.tile([P, S], F32, name=f"result{i}")[:] for i in (2, 3)]
         tots = [keep.tile([P, GROUPS], F32, name=f"tot{i}") for i in range(TILES)]
         invs = [keep.tile([P, GROUPS], F32, name=f"inv{i}") for i in range(TILES)]
 
@@ -123,23 +117,20 @@ def tile_picked_yibm1_post_p_kernel(tc, x_words, x_scales, hT, jump, offs, out):
             jv = jumps[i].rearrange("p (g d) -> p g d", d=D)
             nc.vector.tensor_tensor(out=wts[i][:, gs, 0:D], in0=wts[i][:, gs, 0:D], in1=jv[:, gs, :], op=MULT)
 
-        def total(i, gs):
-            nc.vector.tensor_reduce(out=tots[i][:, gs], in_=wts[i][:, gs, 0 : D + 1], axis=mybir.AxisListType.X, op=ADD)
+        def total(i):
+            nc.vector.tensor_reduce(out=tots[i][:], in_=wts[i][:, :, 0 : D + 1], axis=mybir.AxisListType.X, op=ADD)
 
-        def invert(i, gs):
-            nc.vector.reciprocal(out=invs[i][:, gs], in_=tots[i][:, gs])
+        def invert(i):
+            nc.vector.reciprocal(out=invs[i][:], in_=tots[i][:])
 
-        def share(i, gs):
-            pv = posts[i][:].rearrange("p (g d) -> p g d", d=D)
+        def share(i):
             nc.vector.tensor_tensor(
-                out=pv[:, gs, :],
-                in0=wts[i][:, gs, 0:D],
-                in1=invs[i][:, gs].unsqueeze(2).to_broadcast([P, gs.stop - gs.start, D]),
+                out=posts[i][:].rearrange("p (g d) -> p g d", d=D),
+                in0=wts[i][:, :, 0:D],
+                in1=invs[i][:].unsqueeze(2).to_broadcast([P, GROUPS, D]),
                 op=MULT,
             )
-
-        def logarithm(i, cols):
-            nc.scalar.activation(out=logs[i][:, cols], in_=posts[i][:, cols], func=ACT.Ln, scale=20.0, bias=1.0)
+            nc.scalar.activation(out=logs[i][:], in_=posts[i][:], func=ACT.Ln, scale=20.0, bias=1.0)
 
         def finish(i, cols, engine):
             engine.tensor_tensor(out=results[i][:, cols], in0=posts[i][:, cols], in1=logs[i][:, cols], op=MULT)
@@ -148,29 +139,39 @@ def tile_picked_yibm1_post_p_kernel(tc, x_words, x_scales, hT, jump, offs, out):
         whole = slice(0, S)
         every = slice(0, GROUPS)
         halves = [slice(0, HG), slice(HG, GROUPS)]
-        weigh(0, halves[0])
-        weigh(0, halves[1])
-        weigh(1, every)
-        total(0, every)
-        total(1, every)
-        invert(0, every)
-        invert(1, every)
-        share(0, every)
-        logarithm(0, whole)
+        for i in range(EARLY):
+            interleave(i)
+        for i in (0, 2, 1, 3):
+            quantize(i)
+        for u in range(2):
+            nc.vector.tensor_copy(
+                out=x_codes[:, u * HALF : (u + 1) * HALF],
+                in_=word_table[:].indirect(offsets[:, 16 * u : 16 * (u + 1)]),
+            )
+        for gs in halves:
+            for i in (0, 1):
+                score(i, gs)
+        score(2, every)
+        score(3, every)
+        for gs in halves:
+            for i in (0, 1):
+                weigh(i, gs)
+        total(0)
+        total(1)
+        invert(0)
+        invert(1)
+        share(0)
         weigh(2, every)
-        share(1, every)
-        logarithm(1, whole)
+        share(1)
         weigh(3, every)
-        total(2, every)
-        total(3, every)
-        invert(2, every)
-        invert(3, every)
-        share(2, every)
-        logarithm(2, whole)
-        share(3, every)
-        logarithm(3, whole)
-        finish(0, whole, nc.vector)
-        finish(1, whole, nc.vector)
+        finish(0, whole, nc.gpsimd)
+        finish(1, whole, nc.gpsimd)
+        total(2)
+        total(3)
+        invert(2)
+        invert(3)
+        share(2)
+        share(3)
         finish(2, whole, nc.vector)
         for u in range(2):
             finish(3, slice(u * HALF, (u + 1) * HALF), nc.vector)

@@ -15,15 +15,22 @@ FP8X4 = mybir.dt.float8_e4m3fn_x4
 ACT = mybir.ActivationFunctionType
 MULT = mybir.AluOpType.mult
 ADD = mybir.AluOpType.add
+FREE = mybir.AxisListType.X
 
 P = 128
 PACK = 4
+QUADRANT = 32
+LIST_ROWS = 16
 TILES = V // P
 GROUPS = S // D
-PITCH = 16
 HALF = S // 2
-HG = GROUPS // 2
-EARLY = 4
+NO_WORD = 0.3
+
+PITCH = 16
+PADDED, DENSE = (0, 1), (2, 3)
+
+WEIGH_SPLIT = 384
+FINISH_SPLIT = 384
 
 
 def tile_picked_yibm1_post_p_kernel(tc, x_words, x_scales, hT, jump, offs, out):
@@ -32,41 +39,37 @@ def tile_picked_yibm1_post_p_kernel(tc, x_words, x_scales, hT, jump, offs, out):
         keep = ctx.enter_context(tc.tile_pool(name="keep", bufs=1))
         psum = ctx.enter_context(tc.psum_pool(name="psum", bufs=1))
 
-        offsets = keep.tile([P, S // 16], U16, name="offsets")
+        h_raw = keep.tile([P, PACK, V], F32, name="h_raw")
+        nc.sync.dma_start(out=h_raw[:], in_=hT.rearrange("(p j) t -> p j t", j=PACK))
+        offsets = keep.tile([P, S // LIST_ROWS], U16, name="offsets")
         nc.sync.dma_start(offsets[:], offs)
 
         scale_table = keep.tile([P, T], U8, name="scale_table", align_bytes=64)
         nc.vector.memset(scale_table[:].bitcast(I32), 0)
-        for q in range(4):
+        for q in range(P // QUADRANT):
             nc.scalar.dma_start(
-                out=scale_table[32 * q : 32 * q + 4, :].bitcast(I32),
+                out=scale_table[QUADRANT * q : QUADRANT * q + 4, :].bitcast(I32),
                 in_=x_scales[0, 4 * q : 4 * q + 4, :].bitcast(I32),
             )
 
-        wts = [keep.tile([P, GROUPS, PITCH], F32, name=f"wt{i}", align_bytes=64) for i in range(TILES)]
-        for i in range(TILES):
-            zeros = keep.tile([P, GROUPS], F32, name=f"zeros{i}", tag=f"late{i}", align_bytes=64)
-            nc.vector.memset(zeros[:], 0.0)
-            if i < TILES - 1:
-                nc.vector.tensor_scalar(out=wts[i][:, :, D], in0=zeros[:], scalar1=0.3, scalar2=None, op0=ADD)
-            else:
-                nc.scalar.activation(out=wts[i][:, :, D], in_=zeros[:], func=ACT.Copy, bias=0.3)
+        padded = [keep.tile([P, GROUPS, PITCH], F32, name=f"padded{i}", align_bytes=64) for i in PADDED]
+        zeros_a = keep.tile([P, GROUPS], F32, name="zeros_a", tag="words", align_bytes=64)
+        nc.vector.memset(zeros_a[:], 0.0)
+        nc.vector.tensor_scalar(out=padded[0][:, :, D], in0=zeros_a[:], scalar1=NO_WORD, scalar2=None, op0=ADD)
+        zeros_b = keep.tile([P, GROUPS], F32, name="zeros_b", tag="jump", align_bytes=64)
+        nc.vector.memset(zeros_b[:], 0.0)
+        nc.scalar.activation(out=padded[1][:, :, D], in_=zeros_b[:], func=ACT.Copy, bias=NO_WORD)
 
-        h_rows = hT.rearrange("(p j) t -> p j t", j=PACK)
-        jump_rows = jump.rearrange("(i p) s -> p i s", p=P)
-        h_early = keep.tile([P, PACK, EARLY * P], F32, name="h_early")
-        nc.sync.dma_start(out=h_early[:], in_=h_rows[:, :, 0 : EARLY * P])
-        word_table = keep.tile([P, T], U32, name="word_table", tag="late0", align_bytes=64)
+        word_table = keep.tile([P, T], U32, name="word_table", tag="words", align_bytes=64)
         nc.sync.dma_start(
             out=word_table[:].bitcast(I32),
             in_=x_words[0].rearrange("p n r -> p (n r)").bitcast(I32),
         )
-        jump_early = keep.tile([P, 2, S], F32, name="jump_early", tag="late1", align_bytes=64)
-        nc.sync.dma_start(out=jump_early[:], in_=jump_rows[:, 0:2, :])
-        jump_late = keep.tile([P, 2, S], F32, name="jump_late", tag="late3", align_bytes=64)
-        nc.sync.dma_start(out=jump_late[:], in_=jump_rows[:, 2:4, :])
-        h_raw = [h_early[:, :, i * P : (i + 1) * P] for i in range(EARLY)]
-        jumps = [jump_early[:, 0, :], jump_early[:, 1, :], jump_late[:, 0, :], jump_late[:, 1, :]]
+        jump_rows = jump.rearrange("(i p) s -> p i s", p=P)
+        jump_all = keep.tile([P, TILES, S], F32, name="jump_all", tag="jump", align_bytes=64)
+        nc.sync.dma_start(out=jump_all[:, 0:2, :], in_=jump_rows[:, 0:2, :])
+        nc.sync.dma_start(out=jump_all[:, 2:4, :], in_=jump_rows[:, 2:4, :])
+        jumps = [jump_all[:, i, :] for i in range(TILES)]
 
         x_bytes = keep.tile([P, S], U8, name="x_bytes", align_bytes=64)
         nc.vector.tensor_copy(out=x_bytes[:], in_=scale_table[:].indirect(offsets[:]))
@@ -75,11 +78,30 @@ def tile_picked_yibm1_post_p_kernel(tc, x_words, x_scales, hT, jump, offs, out):
         h_codes = [keep.tile([P, P], U32, name=f"h_codes{i}", align_bytes=64) for i in range(TILES)]
         h_bytes = [keep.tile([P, P], U8, name=f"h_bytes{i}", align_bytes=64) for i in range(TILES)]
         x_codes = keep.tile([P, S], U32, name="x_codes", align_bytes=64)
+        dense_tp = {i: keep.tile([P, S], F32, name=f"tp{i}") for i in DENSE}
+        posts = [keep.tile([P, S], F32, name=f"post{i}") for i in range(TILES)]
+        logs = [keep.tile([P, S], F32, name=f"log{i}") for i in range(TILES)]
+        tots = [keep.tile([P, GROUPS], F32, name=f"tot{i}") for i in range(TILES)]
+        invs = [keep.tile([P, GROUPS], F32, name=f"inv{i}") for i in range(TILES)]
+
+        dense_wt = {2: jumps[1], 3: jumps[0]}
+        reused = padded[1][:].rearrange("p g e -> p (g e)")
+        results = [reused[:, 0:S], reused[:, S : 2 * S]]
+        results = results + [keep.tile([P, S], F32, name=f"result{i}")[:] for i in DENSE]
+
+        def by_group(ap):
+            return ap.rearrange("p (g d) -> p g d", d=D)
+
+        def tp_view(i):
+            return padded[i][:, :, 0:D] if i in PADDED else by_group(dense_tp[i][:])
+
+        def wt_view(i):
+            return padded[i][:, :, 0:D] if i in PADDED else by_group(dense_wt[i])
 
         def interleave(i):
             dst = grouped[i][:].rearrange("p (c e) j -> p c j e", e=4)
-            src = h_raw[i].rearrange("p j (c e) -> p c j e", e=4)
-            if i % 2 == 0:
+            src = h_raw[:, :, i * P : (i + 1) * P].rearrange("p j (c e) -> p c j e", e=4)
+            if i == 0:
                 nc.vector.tensor_copy(out=dst, in_=src)
             else:
                 nc.scalar.copy(out=dst, in_=src)
@@ -91,9 +113,9 @@ def tile_picked_yibm1_post_p_kernel(tc, x_words, x_scales, hT, jump, offs, out):
                 in_=grouped[i][:].rearrange("p c j -> p (c j)"),
             )
 
-        def score(i, gs):
-            cols = slice(gs.start * D, gs.stop * D)
-            bank = psum.tile([P, cols.stop - cols.start], F32, name=f"bank{i}_{gs.start}")
+        def score(i, groups):
+            cols = slice(groups.start * D, groups.stop * D)
+            bank = psum.tile([P, HALF], F32, name=f"bank{i}_{groups.start}")
             nc.tensor.matmul_mx(
                 out=bank[:],
                 lhsT=h_codes[i][:].bitcast(FP8X4),
@@ -103,75 +125,79 @@ def tile_picked_yibm1_post_p_kernel(tc, x_words, x_scales, hT, jump, offs, out):
                 start=True,
                 stop=True,
             )
-            nc.scalar.activation(
-                out=wts[i][:, gs, 0:D], in_=bank[:].rearrange("p (g d) -> p g d", d=D), func=ACT.Exp, scale=0.8
-            )
+            nc.scalar.activation(out=tp_view(i)[:, groups, :], in_=by_group(bank[:]), func=ACT.Exp, scale=0.8)
 
-        posts = [keep.tile([P, S], F32, name=f"post{i}") for i in range(TILES)]
-        logs = [keep.tile([P, S], F32, name=f"log{i}") for i in range(TILES)]
-        results = [jumps[3], jumps[2]] + [keep.tile([P, S], F32, name=f"result{i}")[:] for i in (2, 3)]
-        tots = [keep.tile([P, GROUPS], F32, name=f"tot{i}") for i in range(TILES)]
-        invs = [keep.tile([P, GROUPS], F32, name=f"inv{i}") for i in range(TILES)]
+        def weigh_padded(i, groups):
+            wt = wt_view(i)[:, groups, :]
+            nc.vector.tensor_tensor(out=wt, in0=wt, in1=by_group(jumps[i])[:, groups, :], op=MULT)
 
-        def weigh(i, gs):
-            jv = jumps[i].rearrange("p (g d) -> p g d", d=D)
-            nc.vector.tensor_tensor(out=wts[i][:, gs, 0:D], in0=wts[i][:, gs, 0:D], in1=jv[:, gs, :], op=MULT)
+        def weigh_dense(i, cols, engine):
+            engine.tensor_tensor(out=dense_wt[i][:, cols], in0=dense_tp[i][:, cols], in1=jumps[i][:, cols], op=MULT)
 
         def total(i):
-            nc.vector.tensor_reduce(out=tots[i][:], in_=wts[i][:, :, 0 : D + 1], axis=mybir.AxisListType.X, op=ADD)
+            if i in PADDED:
+                nc.vector.tensor_reduce(out=tots[i][:], in_=padded[i][:, :, 0 : D + 1], axis=FREE, op=ADD)
+            else:
+                sums = keep.tile([P, GROUPS], F32, name=f"sum{i}")
+                nc.vector.tensor_reduce(out=sums[:], in_=wt_view(i), axis=FREE, op=ADD)
+                nc.scalar.activation(out=tots[i][:], in_=sums[:], func=ACT.Copy, bias=NO_WORD)
 
         def invert(i):
             nc.vector.reciprocal(out=invs[i][:], in_=tots[i][:])
 
         def share(i):
             nc.vector.tensor_tensor(
-                out=posts[i][:].rearrange("p (g d) -> p g d", d=D),
-                in0=wts[i][:, :, 0:D],
+                out=by_group(posts[i][:]),
+                in0=wt_view(i),
                 in1=invs[i][:].unsqueeze(2).to_broadcast([P, GROUPS, D]),
                 op=MULT,
             )
             nc.scalar.activation(out=logs[i][:], in_=posts[i][:], func=ACT.Ln, scale=20.0, bias=1.0)
 
-        def finish(i, cols, engine):
-            engine.tensor_tensor(out=results[i][:, cols], in0=posts[i][:, cols], in1=logs[i][:, cols], op=MULT)
-            nc.sync.dma_start(out=out[i * P : (i + 1) * P, cols], in_=results[i][:, cols])
+        def finish(i, cols, engine, result):
+            engine.tensor_tensor(out=result[:, cols], in0=posts[i][:, cols], in1=logs[i][:, cols], op=MULT)
+            nc.sync.dma_start(out=out[i * P : (i + 1) * P, cols], in_=result[:, cols])
 
         whole = slice(0, S)
-        every = slice(0, GROUPS)
-        halves = [slice(0, HG), slice(HG, GROUPS)]
-        for i in range(EARLY):
+        group_halves = [slice(0, GROUPS // 2), slice(GROUPS // 2, GROUPS)]
+
+        for i in range(TILES):
             interleave(i)
-        for i in (0, 2, 1, 3):
+        for i in range(TILES):
             quantize(i)
         for u in range(2):
-            nc.vector.tensor_copy(
-                out=x_codes[:, u * HALF : (u + 1) * HALF],
-                in_=word_table[:].indirect(offsets[:, 16 * u : 16 * (u + 1)]),
-            )
-        for gs in halves:
-            for i in (0, 1):
-                score(i, gs)
-        score(2, every)
-        score(3, every)
-        for gs in halves:
-            for i in (0, 1):
-                weigh(i, gs)
-        total(0)
-        total(1)
-        invert(0)
-        invert(1)
+            list_half = offsets[:, u * HALF // LIST_ROWS : (u + 1) * HALF // LIST_ROWS]
+            nc.vector.tensor_copy(out=x_codes[:, u * HALF : (u + 1) * HALF], in_=word_table[:].indirect(list_half))
+
+        for groups in group_halves:
+            for i in PADDED:
+                score(i, groups)
+        for i in DENSE:
+            for groups in group_halves:
+                score(i, groups)
+        for groups in group_halves:
+            for i in PADDED:
+                weigh_padded(i, groups)
+
+        weigh_dense(2, whole, nc.gpsimd)
+        weigh_dense(3, slice(0, WEIGH_SPLIT), nc.gpsimd)
+        for i in PADDED:
+            total(i)
+        for i in PADDED:
+            invert(i)
         share(0)
-        weigh(2, every)
+        weigh_dense(3, slice(WEIGH_SPLIT, S), nc.vector)
         share(1)
-        weigh(3, every)
-        finish(0, whole, nc.gpsimd)
-        finish(1, whole, nc.gpsimd)
-        total(2)
-        total(3)
-        invert(2)
-        invert(3)
-        share(2)
-        share(3)
-        finish(2, whole, nc.vector)
+
+        finish(0, whole, nc.gpsimd, results[0])
+        finish(1, slice(0, FINISH_SPLIT), nc.gpsimd, results[1])
+        for i in DENSE:
+            total(i)
+        for i in DENSE:
+            invert(i)
+        for i in DENSE:
+            share(i)
+        finish(1, slice(FINISH_SPLIT, S), nc.vector, dense_wt[2])
+        finish(2, whole, nc.vector, results[2])
         for u in range(2):
-            finish(3, slice(u * HALF, (u + 1) * HALF), nc.vector)
+            finish(3, slice(u * HALF, (u + 1) * HALF), nc.vector, results[3])

@@ -29,8 +29,8 @@ NO_WORD = 0.3
 PITCH = 16
 PADDED, DENSE = (0, 1), (2, 3)
 
-WEIGH_SPLIT = 384
-FINISH_SPLIT = 384
+WEIGH_SPLIT = 256
+FINISH_SPLIT = 192
 
 
 def tile_picked_yibm1_post_p_kernel(tc, x_words, x_scales, hT, jump, offs, out):
@@ -75,7 +75,7 @@ def tile_picked_yibm1_post_p_kernel(tc, x_words, x_scales, hT, jump, offs, out):
         nc.vector.tensor_copy(out=x_bytes[:], in_=scale_table[:].indirect(offsets[:]))
 
         grouped = [keep.tile([P, P, PACK], BF16, name=f"h_grouped{i}", align_bytes=64) for i in range(TILES)]
-        h_codes = [keep.tile([P, P], U32, name=f"h_codes{i}", align_bytes=64) for i in range(TILES)]
+        h_codes = {i: keep.tile([P, P], U32, name=f"h_codes{i}", align_bytes=64)[:] for i in PADDED}
         h_bytes = [keep.tile([P, P], U8, name=f"h_bytes{i}", align_bytes=64) for i in range(TILES)]
         x_codes = keep.tile([P, S], U32, name="x_codes", align_bytes=64)
         dense_tp = {i: keep.tile([P, S], F32, name=f"tp{i}") for i in DENSE}
@@ -108,7 +108,7 @@ def tile_picked_yibm1_post_p_kernel(tc, x_words, x_scales, hT, jump, offs, out):
 
         def quantize(i):
             nc.vector.quantize_mx(
-                out=h_codes[i][:].bitcast(FP8X4),
+                out=h_codes[i].bitcast(FP8X4),
                 scales=h_bytes[i][:],
                 in_=grouped[i][:].rearrange("p c j -> p (c j)"),
             )
@@ -118,7 +118,7 @@ def tile_picked_yibm1_post_p_kernel(tc, x_words, x_scales, hT, jump, offs, out):
             bank = psum.tile([P, HALF], F32, name=f"bank{i}_{groups.start}")
             nc.tensor.matmul_mx(
                 out=bank[:],
-                lhsT=h_codes[i][:].bitcast(FP8X4),
+                lhsT=h_codes[i].bitcast(FP8X4),
                 lhsT_scale=h_bytes[i][:],
                 rhs=x_codes[:, cols].bitcast(FP8X4),
                 rhs_scale=x_bytes[:, cols],
@@ -163,11 +163,15 @@ def tile_picked_yibm1_post_p_kernel(tc, x_words, x_scales, hT, jump, offs, out):
 
         for i in range(TILES):
             interleave(i)
-        for i in range(TILES):
+        for i in PADDED:
             quantize(i)
         for u in range(2):
             list_half = offsets[:, u * HALF // LIST_ROWS : (u + 1) * HALF // LIST_ROWS]
             nc.vector.tensor_copy(out=x_codes[:, u * HALF : (u + 1) * HALF], in_=word_table[:].indirect(list_half))
+        late_codes = keep.tile([P, len(DENSE) * P], U32, name="late_codes", tag="words", align_bytes=64)
+        for n, i in enumerate(DENSE):
+            h_codes[i] = late_codes[:, n * P : (n + 1) * P]
+            quantize(i)
 
         for groups in group_halves:
             for i in PADDED:

from contextlib import ExitStack

import concourse.mybir as mybir

K, T, S, V, D = 512, 2048, 512, 512, 8
FLOPS = 2 * K * V * S

F32 = mybir.dt.float32
BF16 = mybir.dt.bfloat16
I32 = mybir.dt.int32
U32 = mybir.dt.uint32
U16 = mybir.dt.uint16
U8 = mybir.dt.uint8
FP8X4 = mybir.dt.float8_e4m3fn_x4
ACT = mybir.ActivationFunctionType
MULT = mybir.AluOpType.mult
ADD = mybir.AluOpType.add
FREE = mybir.AxisListType.X

P = 128
PACK = 4
QUADRANT = 32
LIST_ROWS = 16
TILES = V // P
GROUPS = S // D
HALF = S // 2
NO_WORD = 0.3

PITCH = 16
PADDED, DENSE = (0, 1), (2, 3)

WEIGH_SPLIT = 256
FINISH_SPLIT = 192


def tile_picked_yibm1_post_p_kernel(tc, x_words, x_scales, hT, jump, offs, out):
    nc = tc.nc
    with ExitStack() as ctx:
        keep = ctx.enter_context(tc.tile_pool(name="keep", bufs=1))
        psum = ctx.enter_context(tc.psum_pool(name="psum", bufs=1))

        h_raw = keep.tile([P, PACK, V], F32, name="h_raw")
        nc.sync.dma_start(out=h_raw[:], in_=hT.rearrange("(p j) t -> p j t", j=PACK))
        offsets = keep.tile([P, S // LIST_ROWS], U16, name="offsets")
        nc.sync.dma_start(offsets[:], offs)

        scale_table = keep.tile([P, T], U8, name="scale_table", align_bytes=64)
        nc.vector.memset(scale_table[:].bitcast(I32), 0)
        for q in range(P // QUADRANT):
            nc.scalar.dma_start(
                out=scale_table[QUADRANT * q : QUADRANT * q + 4, :].bitcast(I32),
                in_=x_scales[0, 4 * q : 4 * q + 4, :].bitcast(I32),
            )

        padded = [keep.tile([P, GROUPS, PITCH], F32, name=f"padded{i}", align_bytes=64) for i in PADDED]
        zeros_a = keep.tile([P, GROUPS], F32, name="zeros_a", tag="words", align_bytes=64)
        nc.vector.memset(zeros_a[:], 0.0)
        nc.vector.tensor_scalar(out=padded[0][:, :, D], in0=zeros_a[:], scalar1=NO_WORD, scalar2=None, op0=ADD)
        zeros_b = keep.tile([P, GROUPS], F32, name="zeros_b", tag="jump", align_bytes=64)
        nc.vector.memset(zeros_b[:], 0.0)
        nc.scalar.activation(out=padded[1][:, :, D], in_=zeros_b[:], func=ACT.Copy, bias=NO_WORD)

        word_table = keep.tile([P, T], U32, name="word_table", tag="words", align_bytes=64)
        nc.sync.dma_start(
            out=word_table[:].bitcast(I32),
            in_=x_words[0].rearrange("p n r -> p (n r)").bitcast(I32),
        )
        jump_rows = jump.rearrange("(i p) s -> p i s", p=P)
        jump_all = keep.tile([P, TILES, S], F32, name="jump_all", tag="jump", align_bytes=64)
        nc.sync.dma_start(out=jump_all[:, 0:2, :], in_=jump_rows[:, 0:2, :])
        nc.sync.dma_start(out=jump_all[:, 2:4, :], in_=jump_rows[:, 2:4, :])
        jumps = [jump_all[:, i, :] for i in range(TILES)]

        x_bytes = keep.tile([P, S], U8, name="x_bytes", align_bytes=64)
        nc.vector.tensor_copy(out=x_bytes[:], in_=scale_table[:].indirect(offsets[:]))

        grouped = [keep.tile([P, P, PACK], BF16, name=f"h_grouped{i}", align_bytes=64) for i in range(TILES)]
        h_codes = {i: keep.tile([P, P], U32, name=f"h_codes{i}", align_bytes=64)[:] for i in PADDED}
        h_bytes = [keep.tile([P, P], U8, name=f"h_bytes{i}", align_bytes=64) for i in range(TILES)]
        x_codes = keep.tile([P, S], U32, name="x_codes", align_bytes=64)
        dense_tp = {i: keep.tile([P, S], F32, name=f"tp{i}") for i in DENSE}
        posts = [keep.tile([P, S], F32, name=f"post{i}") for i in range(TILES)]
        logs = [keep.tile([P, S], F32, name=f"log{i}") for i in range(TILES)]
        tots = [keep.tile([P, GROUPS], F32, name=f"tot{i}") for i in range(TILES)]
        invs = [keep.tile([P, GROUPS], F32, name=f"inv{i}") for i in range(TILES)]

        dense_wt = {2: jumps[1], 3: jumps[0]}
        reused = padded[1][:].rearrange("p g e -> p (g e)")
        results = [reused[:, 0:S], reused[:, S : 2 * S]]
        results = results + [keep.tile([P, S], F32, name=f"result{i}")[:] for i in DENSE]

        def by_group(ap):
            return ap.rearrange("p (g d) -> p g d", d=D)

        def tp_view(i):
            return padded[i][:, :, 0:D] if i in PADDED else by_group(dense_tp[i][:])

        def wt_view(i):
            return padded[i][:, :, 0:D] if i in PADDED else by_group(dense_wt[i])

        def interleave(i):
            dst = grouped[i][:].rearrange("p (c e) j -> p c j e", e=4)
            src = h_raw[:, :, i * P : (i + 1) * P].rearrange("p j (c e) -> p c j e", e=4)
            if i == 0:
                nc.vector.tensor_copy(out=dst, in_=src)
            else:
                nc.scalar.copy(out=dst, in_=src)

        def quantize(i):
            nc.vector.quantize_mx(
                out=h_codes[i].bitcast(FP8X4),
                scales=h_bytes[i][:],
                in_=grouped[i][:].rearrange("p c j -> p (c j)"),
            )

        def score(i, groups):
            cols = slice(groups.start * D, groups.stop * D)
            bank = psum.tile([P, HALF], F32, name=f"bank{i}_{groups.start}")
            nc.tensor.matmul_mx(
                out=bank[:],
                lhsT=h_codes[i].bitcast(FP8X4),
                lhsT_scale=h_bytes[i][:],
                rhs=x_codes[:, cols].bitcast(FP8X4),
                rhs_scale=x_bytes[:, cols],
                start=True,
                stop=True,
            )
            nc.scalar.activation(out=tp_view(i)[:, groups, :], in_=by_group(bank[:]), func=ACT.Exp, scale=0.8)

        def weigh_padded(i, groups):
            wt = wt_view(i)[:, groups, :]
            nc.vector.tensor_tensor(out=wt, in0=wt, in1=by_group(jumps[i])[:, groups, :], op=MULT)

        def weigh_dense(i, cols, engine):
            engine.tensor_tensor(out=dense_wt[i][:, cols], in0=dense_tp[i][:, cols], in1=jumps[i][:, cols], op=MULT)

        def total(i):
            if i in PADDED:
                nc.vector.tensor_reduce(out=tots[i][:], in_=padded[i][:, :, 0 : D + 1], axis=FREE, op=ADD)
            else:
                sums = keep.tile([P, GROUPS], F32, name=f"sum{i}")
                nc.vector.tensor_reduce(out=sums[:], in_=wt_view(i), axis=FREE, op=ADD)
                nc.scalar.activation(out=tots[i][:], in_=sums[:], func=ACT.Copy, bias=NO_WORD)

        def invert(i):
            nc.vector.reciprocal(out=invs[i][:], in_=tots[i][:])

        def share(i):
            nc.vector.tensor_tensor(
                out=by_group(posts[i][:]),
                in0=wt_view(i),
                in1=invs[i][:].unsqueeze(2).to_broadcast([P, GROUPS, D]),
                op=MULT,
            )
            nc.scalar.activation(out=logs[i][:], in_=posts[i][:], func=ACT.Ln, scale=20.0, bias=1.0)

        def finish(i, cols, engine, result):
            engine.tensor_tensor(out=result[:, cols], in0=posts[i][:, cols], in1=logs[i][:, cols], op=MULT)
            nc.sync.dma_start(out=out[i * P : (i + 1) * P, cols], in_=result[:, cols])

        whole = slice(0, S)
        group_halves = [slice(0, GROUPS // 2), slice(GROUPS // 2, GROUPS)]

        for i in range(TILES):
            interleave(i)
        for i in PADDED:
            quantize(i)
        for u in range(2):
            list_half = offsets[:, u * HALF // LIST_ROWS : (u + 1) * HALF // LIST_ROWS]
            nc.vector.tensor_copy(out=x_codes[:, u * HALF : (u + 1) * HALF], in_=word_table[:].indirect(list_half))
        late_codes = keep.tile([P, len(DENSE) * P], U32, name="late_codes", tag="words", align_bytes=64)
        for n, i in enumerate(DENSE):
            h_codes[i] = late_codes[:, n * P : (n + 1) * P]
            quantize(i)

        for groups in group_halves:
            for i in PADDED:
                score(i, groups)
        for i in DENSE:
            for groups in group_halves:
                score(i, groups)
        for groups in group_halves:
            for i in PADDED:
                weigh_padded(i, groups)

        weigh_dense(2, whole, nc.gpsimd)
        weigh_dense(3, slice(0, WEIGH_SPLIT), nc.gpsimd)
        for i in PADDED:
            total(i)
        for i in PADDED:
            invert(i)
        share(0)
        weigh_dense(3, slice(WEIGH_SPLIT, S), nc.vector)
        share(1)

        finish(0, whole, nc.gpsimd, results[0])
        finish(1, slice(0, FINISH_SPLIT), nc.gpsimd, results[1])
        for i in DENSE:
            total(i)
        for i in DENSE:
            invert(i)
        for i in DENSE:
            share(i)
        finish(1, slice(FINISH_SPLIT, S), nc.vector, dense_wt[2])
        finish(2, whole, nc.vector, results[2])
        for u in range(2):
            finish(3, slice(u * HALF, (u + 1) * HALF), nc.vector, results[3])
